import numpy as np
import ml_dtypes


def mxq(x, axis, fmt="e4m3"):
    dtype, down = {"e4m3": (ml_dtypes.float8_e4m3fn, 7), "e5m2": (ml_dtypes.float8_e5m2, 14)}[fmt]
    v = np.moveaxis(np.asarray(x, np.float32).astype(ml_dtypes.bfloat16).astype(np.float64), axis, -1)
    blocks = v.reshape(v.shape[:-1] + (-1, 32))
    amax = np.abs(blocks).max(-1, keepdims=True)
    byte = np.maximum(np.where(amax > 0, np.frexp(amax)[1] - 1 + 127, 0) - down, 1)
    scale = np.exp2(byte - 127.0)
    codes = (blocks / scale).astype(np.float32).astype(dtype).astype(np.float64)
    return np.moveaxis((codes * scale).reshape(v.shape), -1, axis)


WIDE = False


def mx_kscale(k):
    if not WIDE:
        return np.ones(k)
    levels = np.array([30, -30])
    if k % 512:
        return np.exp2(np.random.permutation(np.resize(levels, k // 32))).repeat(32)
    a = np.empty((k // 512, 16))
    for p in range(k // 512):
        a[p, :8] = np.random.permutation(np.resize(levels, 8))
        for g in range(8):
            far = levels[np.abs(levels - a[p, g]) >= 10]
            a[p, g + 8] = far[np.random.randint(len(far))]
    return np.exp2(a.ravel()).repeat(32)


BF16 = ml_dtypes.bfloat16


def bf(x):
    return np.asarray(x, np.float32).astype(BF16)


def f64(x):
    return np.asarray(x).astype(np.float64)


E2M1 = np.array([0.0, 0.5, 1.0, 1.5, 2.0, 3.0, 4.0, 6.0, -0.0, -0.5, -1.0, -1.5, -2.0, -3.0, -4.0, -6.0])


def pack_weight(w, fmt):
    k, n = w.shape
    w = f64(bf(w)).reshape(k // 32, 32, n)
    amax = np.abs(w).max(1)
    if fmt == "e4m3":
        byte = np.frexp(amax)[1] - 1 + 127 - 7
    else:
        mant, ex = np.frexp(amax / 6.0)
        byte = np.where(mant > 0.5, ex, ex - 1) + 127
    byte = np.clip(np.where(amax > 0, byte, 1), 1, 254)
    scaled = (w * np.exp2(127.0 - byte)[:, None, :]).reshape(k, n).astype(np.float32)
    by_word = np.ascontiguousarray(scaled.reshape(k // 512, 128, 4, n).transpose(0, 1, 3, 2))
    if fmt == "e4m3":
        words = by_word.astype(ml_dtypes.float8_e4m3fn).view(np.uint8)
    else:
        c = by_word.astype(ml_dtypes.float4_e2m1fn).view(np.uint8) & 0xF
        words = c[..., 0::2] | (c[..., 1::2] << 4)
    return np.ascontiguousarray(words), np.ascontiguousarray(byte.astype(np.uint8).reshape(k // 512, 16, n))


def unpack_weight(words, scales, fmt):
    g, p, n, _ = words.shape
    if fmt == "e4m3":
        vals = np.ascontiguousarray(words).view(ml_dtypes.float8_e4m3fn).astype(np.float64)
    else:
        nib = np.empty((g, p, n, 4), np.uint8)
        nib[..., 0::2] = words & 0xF
        nib[..., 1::2] = words >> 4
        vals = E2M1[nib]
    vals = vals * np.repeat(np.exp2(scales.astype(np.float64) - 127.0), 8, axis=1)[..., None]
    return vals.transpose(0, 1, 3, 2).reshape(g * 512, n)
def pack4(w):
    words, scales = pack_weight(w, "e2m1")
    return words.reshape(words.shape[0], 128, -1), scales


def unpack4(words, scales):
    return unpack_weight(words.reshape(words.shape[0], 128, -1, 2), scales, "e2m1")


UNITS, T = 1536, 1024


def setup_inputs():
    s = mx_kscale(T)
    u = mx_kscale(UNITS)
    w = np.random.standard_normal((T, T)) / np.sqrt(T) / s[:, None]
    w_words, w_scales = pack4(w)
    return {
        "y": bf(np.random.standard_normal((UNITS, T)) * s),
        "w_words": w_words,
        "w_scales": w_scales,
        "v": bf(np.random.standard_normal((UNITS, UNITS)) / np.sqrt(UNITS) / u),
        "dates": bf(np.random.uniform(0, 1, (T,))),
        "starts": bf(np.random.uniform(0.1, 0.9, (UNITS,))),
        "treated": bf((1 + 0.1 * np.random.standard_normal((UNITS,))) * u),
        "control": bf((-0.6 + 0.1 * np.random.standard_normal((UNITS,))) * u),
    }


def reference(y, w_words, w_scales, v, dates, starts, treated, control):
    r = mxq(f64(y), 1, "e4m3") @ unpack4(w_words, w_scales)
    on = f64(dates)[None, :] >= f64(starts)[:, None]
    c = np.where(on, f64(treated)[:, None], f64(control)[:, None])
    e = r * c
    return mxq(f64(v), 1, "e4m3") @ mxq(e, 0, "e5m2")

@@ -1,0 +1,312 @@
+from contextlib import ExitStack
+
+import concourse.mybir as mybir
+from concourse.masks import make_identity
+
+UNITS, T = 1536, 1024
+FLOPS = 2 * UNITS * T * T + 2 * UNITS * UNITS * T
+
+F32 = mybir.dt.float32
+BF16 = mybir.dt.bfloat16
+U32 = mybir.dt.uint32
+I32 = mybir.dt.int32
+U8 = mybir.dt.uint8
+E4M3 = mybir.dt.float8_e4m3fn_x4
+E5M2 = mybir.dt.float8_e5m2_x4
+E2M1 = mybir.dt.float4_e2m1fn_x4
+OP = mybir.AluOpType
+ACT = mybir.ActivationFunctionType
+
+P = 128
+G = UNITS // 512
+H = T // 512
+
+
+def tile_staggered_adoption_weighted_panel_s9_kernel(
+    tc, y, w_words, w_scales, v, dates, starts, treated, control, out
+):
+    nc = tc.nc
+    with ExitStack() as ctx:
+        keep = ctx.enter_context(tc.tile_pool(name="keep", bufs=1))
+        work = ctx.enter_context(tc.tile_pool(name="work", bufs=3))
+        psum = ctx.enter_context(tc.psum_pool(name="psum", bufs=4))
+        ctx.enter_context(tc.manual_schedule())
+
+        ident = keep.tile([P, P], F32, name="ident")
+        ident_bf = keep.tile([P, P], BF16, name="ident_bf")
+        dcol = keep.tile([P, 8], BF16, name="dcol")
+        ucol = [keep.tile([P, G, 4], BF16, name=f"ucol{i}") for i in range(3)]
+        wsc = keep.tile([P, H, T], U8, name="wsc", align_bytes=64)
+        wt = keep.tile([P, H, 2 * T], U8, name="wt", align_bytes=64)
+        yraw = [keep.tile([P, 4, T], BF16, name=f"yraw{g}", align_bytes=64) for g in range(G)]
+        vraw = [keep.tile([P, 4, UNITS], BF16, name=f"vraw{q}", align_bytes=64) for q in range(3)]
+
+        y_v = y.rearrange("(g p t) k -> g p t k", p=P, t=4)
+        v_v = v.rearrange("(q m p) k -> q p m k", p=P, m=4)
+        w_v = w_words.rearrange("h p n -> p h n")
+
+        def load_y(g, t0, t1):
+            nc.sync.dma_start(out=yraw[g][:, t0:t1, :], in_=y_v[g, :, t0:t1, :])
+
+        def load_w(c):
+            cols = slice(T * c, T * (c + 1))
+            nc.sync.dma_start(out=wt[:, :, cols].bitcast(I32), in_=w_v[:, :, cols].bitcast(I32))
+
+        def load_v(q, a):
+            nc.sync.dma_start(out=vraw[q][:, 2 * a : 2 * a + 2, :], in_=v_v[q, :, 2 * a : 2 * a + 2, :])
+
+        vec = nc.vector
+        make_identity(nc, ident[:])
+        nc.scalar.dma_start(out=dcol[:], in_=dates.rearrange("(p m) -> p m", m=8))
+        load_y(0, 0, 1)
+        for dst, src, queue in zip(ucol, (starts, treated, control), (nc.scalar, nc.gpsimd, nc.gpsimd)):
+            queue.dma_start(out=dst[:], in_=src.rearrange("(g p t) -> p g t", p=P, t=4))
+        load_y(0, 1, 2)
+        vec.memset(wsc[:].rearrange("p h n -> p (h n)").bitcast(I32), 0)
+        ws_v = w_scales.rearrange("h (q r) n -> r q h n", r=4)
+        for r in range(4):
+            nc.scalar.dma_start(out=wsc[r:P:32, :, :].bitcast(I32), in_=ws_v[r].bitcast(I32))
+        load_y(0, 2, 3)
+        load_y(0, 3, 4)
+        load_w(0)
+        load_w(1)
+        load_y(1, 0, 2)
+        load_y(1, 2, 4)
+        load_v(0, 0)
+        load_v(0, 1)
+        load_y(2, 0, 2)
+        load_y(2, 2, 4)
+        for q in (1, 2):
+            load_v(q, 0)
+            load_v(q, 1)
+
+        vec.tensor_copy(out=ident_bf[:], in_=ident[:])
+        dps = psum.tile([P, 8, P], BF16, name="dps", tag="tp")
+        for m in range(8):
+            nc.tensor.transpose(dps[:, m, :], dcol[:, m : m + 1].to_broadcast([P, P]), ident_bf[:])
+        dall = keep.tile([P, T], BF16, name="dall", align_bytes=64)
+        vec.tensor_copy(out=dall[:].rearrange("p (j m) -> p j m", m=8), in_=dps[:].rearrange("p m j -> p j m"))
+
+        s_c, t_c, c_c = [u[:].rearrange("p g t -> p (g t)") for u in ucol]
+
+        def col(name):
+            return keep.tile([P, 4 * G], F32, name=name)
+
+        abs_t, abs_c, abs_s = col("abs_t"), col("abs_c"), col("abs_s")
+        diff, flag, thr0, sign, flagn = col("diff"), col("flag"), col("thr0"), col("sign"), col("flagn")
+        part, gain, part2, thr, base = col("part"), col("gain"), col("part2"), col("thr"), col("base")
+        for dst, src in ((abs_s, s_c), (abs_t, t_c), (abs_c, c_c)):
+            vec.scalar_tensor_tensor(out=dst[:], in0=src, scalar=-1.0, in1=src, op0=OP.mult, op1=OP.max)
+        vec.tensor_tensor(out=diff[:], in0=t_c, in1=c_c, op=OP.subtract)
+        vec.tensor_tensor(out=flag[:], in0=abs_t[:], in1=abs_c[:], op=OP.is_ge)
+        vec.scalar_tensor_tensor(out=thr0[:], in0=abs_s[:], scalar=-(2.0**-10), in1=s_c, op0=OP.mult, op1=OP.add)
+        vec.tensor_scalar(out=sign[:], in0=flag[:], scalar1=2.0, scalar2=-1.0, op0=OP.mult, op1=OP.add)
+        vec.tensor_scalar(out=flagn[:], in0=flag[:], scalar1=-1.0, scalar2=1.0, op0=OP.mult, op1=OP.add)
+        vec.tensor_tensor(out=part[:], in0=flag[:], in1=c_c, op=OP.mult)
+        vec.tensor_tensor(out=gain[:], in0=diff[:], in1=sign[:], op=OP.mult)
+        vec.tensor_tensor(out=part2[:], in0=flagn[:], in1=t_c, op=OP.mult)
+        vec.scalar_tensor_tensor(out=thr[:], in0=thr0[:], scalar=-(2.0**-120), in1=sign[:], op0=OP.add, op1=OP.mult)
+        vec.tensor_tensor(out=base[:], in0=part[:], in1=part2[:], op=OP.add)
+
+        cw = [keep.tile([P, 4, T], BF16, name=f"cw{g}", align_bytes=64) for g in range(G)]
+
+        def mask(g, t):
+            i = 4 * g + t
+            mk = work.tile([P, T], BF16, name="mk", align_bytes=64)
+            vec.tensor_scalar(
+                out=mk[:], in0=dall[:], scalar1=sign[:, i : i + 1], scalar2=thr[:, i : i + 1], op0=OP.mult, op1=OP.is_ge
+            )
+            return mk
+
+        def affine(g, t, mk, engine):
+            i = 4 * g + t
+            dst, ga, ba = cw[g][:, t, :], gain[:, i : i + 1], base[:, i : i + 1]
+            if engine == "V":
+                vec.tensor_scalar(out=dst, in0=mk[:], scalar1=ga, scalar2=ba, op0=OP.mult, op1=OP.add)
+            else:
+                nc.scalar.activation(out=dst, in_=mk[:], func=ACT.Identity, bias=ba, scale=ga)
+
+        ycodes = [keep.tile([P, 2048 // 2], U32, name=f"yc{g}", align_bytes=64) for g in range(G)]
+        yscales = [keep.tile([P, 2048 // 2], U8, name=f"ys{g}", align_bytes=64) for g in range(G)]
+        vcodes, ecodes, egrp, preps = {}, {}, {}, {}
+
+        def blocks(op):
+            kind, i, j = op[:3]
+            if kind == "y":
+                return yraw[i][:].bitcast(F32)[:, 2 * j : 2 * j + 2, :].rearrange("p t (h k) -> p (t h) k", h=H)
+            return vraw[i][:].bitcast(F32)[:, :, 256 * j : 256 * (j + 1)]
+
+        def prep(op):
+            engine = op[3]
+            if engine:
+                ordered = work.tile([P, 4, 2, P], F32, name="ordered", align_bytes=64, bufs=2)
+                copy = vec.tensor_copy if engine == "V" else nc.scalar.copy
+                copy(out=ordered[:], in_=blocks(op).rearrange("p s (w u) -> p s u w", u=2))
+                preps[op] = ordered
+
+        def turn(op):
+            banks = []
+            src = blocks(op)
+            for b in range(2):
+                bank = psum.tile([P, 512], F32, name="tp")
+                for s in range(2):
+                    for u in range(2):
+                        words = preps[op][:, 2 * b + s, u, :] if op in preps else src[:, 2 * b + s, u:256:2]
+                        nc.tensor.transpose(bank[:, P * (2 * s + u) : P * (2 * s + u + 1)], words, ident[:])
+                banks.append(bank)
+            return banks
+
+        def fetch_bank(dst, bank, engine):
+            copy = vec.tensor_copy if engine == "V" else nc.scalar.copy
+            copy(
+                out=dst.bitcast(F32).rearrange("p (a r u) -> p a r u", a=2, u=2),
+                in_=bank[:].rearrange("p (a u r) -> p a r u", a=2, u=2),
+            )
+
+        def fetch(op, banks):
+            grp = work.tile([P, 2048], BF16, name="grp", align_bytes=64, bufs=6)
+            for b in range(2):
+                fetch_bank(grp[:, 1024 * b : 1024 * (b + 1)], banks[b], op[4][b])
+            return grp
+
+        def quant(op, grp):
+            kind, i, j = op[:3]
+            if kind == "y":
+                codes, scales = ycodes[i][:, 512 * j : 512 * (j + 1)], yscales[i][:, 512 * j : 512 * (j + 1)]
+            else:
+                ct = keep.tile([P, 512], U32, name=f"vc{i}{j}", align_bytes=64)
+                st = keep.tile([P, 512], U8, name=f"vs{i}{j}", align_bytes=64)
+                vcodes[i, j] = (ct, st)
+                codes, scales = ct[:], st[:]
+            vec.quantize_mx(out=codes.bitcast(E4M3), scales=scales, in_=grp[:])
+
+        def first(g, jcs, ts, banks):
+            for t in ts:
+                for jc in jcs:
+                    for h in range(H):
+                        m = slice(256 * t + P * h, 256 * t + P * (h + 1))
+                        nc.tensor.matmul_mx(
+                            out=banks[jc][:, t, :],
+                            lhsT=ycodes[g][:, m].bitcast(E4M3),
+                            lhsT_scale=yscales[g][:, m],
+                            rhs=wt[:, h, 256 * jc : 256 * (jc + 1)].bitcast(E2M1),
+                            rhs_scale=wsc[:, h, P * jc : P * (jc + 1)],
+                            start=(h == 0),
+                            stop=(h == H - 1),
+                        )
+
+        def weigh(g, jc, bank):
+            if jc % 4 == 0:
+                egrp[g, jc // 4] = work.tile([P, 512, 4], BF16, name="eg", align_bytes=64)
+            j = P * (jc % 4)
+            vec.tensor_tensor(
+                out=egrp[g, jc // 4][:, j : j + P, :],
+                in0=bank[:].rearrange("p t n -> p n t"),
+                in1=cw[g][:, :, P * jc : P * (jc + 1)].rearrange("p t n -> p n t"),
+                op=OP.mult,
+            )
+
+        def quant_e(g, half):
+            ct = keep.tile([P, 512], U32, name=f"ec{g}{half}", align_bytes=64)
+            st = keep.tile([P, 512], U8, name=f"es{g}{half}", align_bytes=64)
+            ecodes[g, half] = (ct, st)
+            vec.quantize_mx(out=ct[:].bitcast(E5M2), scales=st[:], in_=egrp[g, half][:].rearrange("p n t -> p (n t)"))
+
+        def second(m, half, tag):
+            q, mi = m // 4, m % 4
+            bank = psum.tile([P, 512], F32, name="bank2", tag=tag)
+            for g in range(G):
+                codes, scales = vcodes[q, g]
+                ec, es = ecodes[g, half]
+                nc.tensor.matmul_mx(
+                    out=bank[:],
+                    lhsT=codes[:, P * mi : P * (mi + 1)].bitcast(E4M3),
+                    lhsT_scale=scales[:, P * mi : P * (mi + 1)],
+                    rhs=ec[:].bitcast(E5M2),
+                    rhs_scale=es[:],
+                    start=(g == 0),
+                    stop=(g == G - 1),
+                )
+            return bank
+
+        def acc_banks(jcs):
+            return {jc: psum.tile([P, 4, P], F32, name="acc") for jc in jcs}
+
+        banks = acc_banks(range(4))
+        src = yraw[0][:].bitcast(F32)
+        grp0 = []
+        for t in range(4):
+            tb = psum.tile([P, 512], F32, name="tp")
+            for s in range(4):
+                h, u = s // 2, s % 2
+                nc.tensor.transpose(tb[:, P * s : P * (s + 1)], src[:, t, 256 * h + u : 256 * (h + 1) : 2], ident[:])
+            gt = work.tile([P, 1024], BF16, name="grp0", align_bytes=64, bufs=4)
+            fetch_bank(gt[:], tb, "SSSS"[t])
+            grp0.append(gt)
+        for t in range(4):
+            mk = mask(0, t)
+            cols = slice(256 * t, 256 * (t + 1))
+            vec.quantize_mx(out=ycodes[0][:, cols].bitcast(E4M3), scales=yscales[0][:, cols], in_=grp0[t][:])
+            affine(0, t, mk, "V")
+            first(0, range(4), (t,), banks)
+
+        stage1 = [
+            ("y", 1, 0, None, "SS", 0), ("y", 1, 1, None, "SS", 0), None, ("v", 0, 0, None, "SS", 0),
+            ("y", 2, 0, None, "SS", 0), ("y", 2, 1, None, "SS", 0), ("v", 0, 1, None, "SS", 0), ("v", 0, 2, None, "SS", 0),
+            ("v", 1, 0, None, "SS", 1), ("v", 1, 1, None, "SS", 1), ("v", 1, 2, None, "SS", 1), None,
+        ]
+        stage2 = {4: ("v", 2, 0, "S", "SV", 1), 7: ("v", 2, 1, "S", "SV", 1), 10: ("v", 2, 2, "S", "SV", 1)}
+        pending, late = [], []
+        order = [op for op in stage1 if op] + [op for op in stage2.values()]
+        turned = []
+
+        def start_op(op):
+            if op:
+                (late if op[5] else pending).append((op, fetch(op, turn(op))))
+                turned.append(op)
+                if len(turned) < len(order):
+                    prep(order[len(turned)])
+
+        prep(order[0])
+        aff = [(g, t) for g in (1, 2) for t in range(4)]
+        groups = [(0, (0, 1)), (0, (2, 3)), (0, (4, 5)), (0, (6, 7))] + [(g, (j, j + 1)) for g in (1, 2) for j in (0, 2, 4, 6)]
+        ready_e = []
+        for k, (g, (ja, jb)) in enumerate(groups):
+            if k >= 2:
+                banks = acc_banks((ja, jb))
+                first(g, (ja,), range(4), banks)
+                first(g, (jb,), range(4), banks)
+            job = aff.pop(0) if aff else None
+            if job:
+                mk = mask(*job)
+            weigh(g, ja, banks[ja])
+            if ready_e:
+                quant_e(*ready_e.pop())
+            if pending:
+                quant(*pending.pop(0))
+            start_op(stage1[k])
+            if job:
+                affine(*job, mk, "SSSSSSSSSSSS"[k])
+            weigh(g, jb, banks[jb])
+            if jb % 4 == 3:
+                ready_e.append((g, jb // 4))
+        quant_e(*ready_e.pop())
+
+        out_v = out.rearrange("(m p) j -> m p j", p=P)
+        outs = {}
+        steps = [(m, half) for mp in range(6) for half in range(2) for m in (2 * mp, 2 * mp + 1)]
+        for i, (m, half) in enumerate(steps):
+            bank = second(m, half, "acc" if i < 14 or i % 2 == 0 else "tp")
+            if i in stage2:
+                start_op(stage2[i])
+            if m not in outs:
+                outs[m] = work.tile([P, T], F32, name="o", align_bytes=64, bufs=5)
+            cols = slice(512 * half, 512 * (half + 1))
+            copy = nc.scalar.copy if i % 2 == 0 else vec.tensor_copy
+            copy(out=outs[m][:, cols], in_=bank[:])
+            if late or pending:
+                quant(*(pending or late).pop(0))
+            if m >= 10:
+                nc.sync.dma_start(out=out_v[m, :, cols], in_=outs[m][:, cols])
+            elif half == 1:
+                nc.sync.dma_start(out=out_v[m], in_=outs[m][:])

@@ -59,15 +59,15 @@ def tile_staggered_adoption_weighted_panel_s9_kernel(
         make_identity(nc, ident[:])
         nc.scalar.dma_start(out=dcol[:], in_=dates.rearrange("(p m) -> p m", m=8))
         load_y(0, 0, 1)
-        for dst, src, queue in zip(ucol, (starts, treated, control), (nc.scalar, nc.gpsimd, nc.gpsimd)):
+        for dst, src, queue in zip(ucol, (starts, treated, control), (nc.scalar, nc.scalar, nc.scalar)):
             queue.dma_start(out=dst[:], in_=src.rearrange("(g p t) -> p g t", p=P, t=4))
         load_y(0, 1, 2)
+        load_y(0, 2, 3)
+        load_y(0, 3, 4)
         vec.memset(wsc[:].rearrange("p h n -> p (h n)").bitcast(I32), 0)
         ws_v = w_scales.rearrange("h (q r) n -> r q h n", r=4)
         for r in range(4):
             nc.scalar.dma_start(out=wsc[r:P:32, :, :].bitcast(I32), in_=ws_v[r].bitcast(I32))
-        load_y(0, 2, 3)
-        load_y(0, 3, 4)
         load_w(0)
         load_w(1)
         load_y(1, 0, 2)
@@ -86,27 +86,6 @@ def tile_staggered_adoption_weighted_panel_s9_kernel(
             nc.tensor.transpose(dps[:, m, :], dcol[:, m : m + 1].to_broadcast([P, P]), ident_bf[:])
         dall = keep.tile([P, T], BF16, name="dall", align_bytes=64)
         vec.tensor_copy(out=dall[:].rearrange("p (j m) -> p j m", m=8), in_=dps[:].rearrange("p m j -> p j m"))
-
-        s_c, t_c, c_c = [u[:].rearrange("p g t -> p (g t)") for u in ucol]
-
-        def col(name):
-            return keep.tile([P, 4 * G], F32, name=name)
-
-        abs_t, abs_c, abs_s = col("abs_t"), col("abs_c"), col("abs_s")
-        diff, flag, thr0, sign, flagn = col("diff"), col("flag"), col("thr0"), col("sign"), col("flagn")
-        part, gain, part2, thr, base = col("part"), col("gain"), col("part2"), col("thr"), col("base")
-        for dst, src in ((abs_s, s_c), (abs_t, t_c), (abs_c, c_c)):
-            vec.scalar_tensor_tensor(out=dst[:], in0=src, scalar=-1.0, in1=src, op0=OP.mult, op1=OP.max)
-        vec.tensor_tensor(out=diff[:], in0=t_c, in1=c_c, op=OP.subtract)
-        vec.tensor_tensor(out=flag[:], in0=abs_t[:], in1=abs_c[:], op=OP.is_ge)
-        vec.scalar_tensor_tensor(out=thr0[:], in0=abs_s[:], scalar=-(2.0**-10), in1=s_c, op0=OP.mult, op1=OP.add)
-        vec.tensor_scalar(out=sign[:], in0=flag[:], scalar1=2.0, scalar2=-1.0, op0=OP.mult, op1=OP.add)
-        vec.tensor_scalar(out=flagn[:], in0=flag[:], scalar1=-1.0, scalar2=1.0, op0=OP.mult, op1=OP.add)
-        vec.tensor_tensor(out=part[:], in0=flag[:], in1=c_c, op=OP.mult)
-        vec.tensor_tensor(out=gain[:], in0=diff[:], in1=sign[:], op=OP.mult)
-        vec.tensor_tensor(out=part2[:], in0=flagn[:], in1=t_c, op=OP.mult)
-        vec.scalar_tensor_tensor(out=thr[:], in0=thr0[:], scalar=-(2.0**-120), in1=sign[:], op0=OP.add, op1=OP.mult)
-        vec.tensor_tensor(out=base[:], in0=part[:], in1=part2[:], op=OP.add)
 
         cw = [keep.tile([P, 4, T], BF16, name=f"cw{g}", align_bytes=64) for g in range(G)]
 
@@ -200,9 +179,9 @@ def tile_staggered_adoption_weighted_panel_s9_kernel(
                 egrp[g, jc // 4] = work.tile([P, 512, 4], BF16, name="eg", align_bytes=64)
             j = P * (jc % 4)
             vec.tensor_tensor(
-                out=egrp[g, jc // 4][:, j : j + P, :],
-                in0=bank[:].rearrange("p t n -> p n t"),
-                in1=cw[g][:, :, P * jc : P * (jc + 1)].rearrange("p t n -> p n t"),
+                out=egrp[g, jc // 4][:, j : j + P, :].rearrange("p (c i) t -> p c t i", i=4),
+                in0=bank[:].rearrange("p t (c i) -> p c t i", i=4),
+                in1=cw[g][:, :, P * jc : P * (jc + 1)].rearrange("p t (c i) -> p c t i", i=4),
                 op=OP.mult,
             )
 
@@ -243,19 +222,44 @@ def tile_staggered_adoption_weighted_panel_s9_kernel(
             gt = work.tile([P, 1024], BF16, name="grp0", align_bytes=64, bufs=4)
             fetch_bank(gt[:], tb, "SSSS"[t])
             grp0.append(gt)
-        for t in range(4):
-            mk = mask(0, t)
+        def quant0(t):
             cols = slice(256 * t, 256 * (t + 1))
             vec.quantize_mx(out=ycodes[0][:, cols].bitcast(E4M3), scales=yscales[0][:, cols], in_=grp0[t][:])
-            affine(0, t, mk, "V")
             first(0, range(4), (t,), banks)
 
-        stage1 = [
-            ("y", 1, 0, None, "SS", 0), ("y", 1, 1, None, "SS", 0), None, ("v", 0, 0, None, "SS", 0),
-            ("y", 2, 0, None, "SS", 0), ("y", 2, 1, None, "SS", 0), ("v", 0, 1, None, "SS", 0), ("v", 0, 2, None, "SS", 0),
-            ("v", 1, 0, None, "SS", 1), ("v", 1, 1, None, "SS", 1), ("v", 1, 2, None, "SS", 1), None,
-        ]
-        stage2 = {4: ("v", 2, 0, "S", "SV", 1), 7: ("v", 2, 1, "S", "SV", 1), 10: ("v", 2, 2, "S", "SV", 1)}
+        quant0(0)
+        s_c, t_c, c_c = [u[:].rearrange("p g t -> p (g t)") for u in ucol]
+
+        def col(name):
+            return keep.tile([P, 4 * G], F32, name=name)
+
+        abs_t, abs_c, abs_s = col("abs_t"), col("abs_c"), col("abs_s")
+        diff, flag, thr0, sign, flagn = col("diff"), col("flag"), col("thr0"), col("sign"), col("flagn")
+        part, gain, part2, thr, base = col("part"), col("gain"), col("part2"), col("thr"), col("base")
+        for dst, src in ((abs_s, s_c), (abs_t, t_c), (abs_c, c_c)):
+            vec.scalar_tensor_tensor(out=dst[:], in0=src, scalar=-1.0, in1=src, op0=OP.mult, op1=OP.max)
+        vec.tensor_tensor(out=diff[:], in0=t_c, in1=c_c, op=OP.subtract)
+        vec.tensor_tensor(out=flag[:], in0=abs_t[:], in1=abs_c[:], op=OP.is_ge)
+        vec.scalar_tensor_tensor(out=thr0[:], in0=abs_s[:], scalar=-(2.0**-10), in1=s_c, op0=OP.mult, op1=OP.add)
+        vec.tensor_scalar(out=sign[:], in0=flag[:], scalar1=2.0, scalar2=-1.0, op0=OP.mult, op1=OP.add)
+        vec.tensor_scalar(out=flagn[:], in0=flag[:], scalar1=-1.0, scalar2=1.0, op0=OP.mult, op1=OP.add)
+        vec.tensor_tensor(out=part[:], in0=flag[:], in1=c_c, op=OP.mult)
+        vec.tensor_tensor(out=gain[:], in0=diff[:], in1=sign[:], op=OP.mult)
+        vec.tensor_tensor(out=part2[:], in0=flagn[:], in1=t_c, op=OP.mult)
+        vec.scalar_tensor_tensor(out=thr[:], in0=thr0[:], scalar=-(2.0**-120), in1=sign[:], op0=OP.add, op1=OP.mult)
+        vec.tensor_tensor(out=base[:], in0=part[:], in1=part2[:], op=OP.add)
+        quant0(1)
+        m0, m1 = mask(0, 0), mask(0, 1)
+        affine(0, 0, m0, "V")
+        affine(0, 1, m1, "S")
+        quant0(2)
+        m2, m3 = mask(0, 2), mask(0, 3)
+        quant0(3)
+        affine(0, 2, m2, "V")
+        affine(0, 3, m3, "V")
+
+        stage1 = [('y', 1, 0, 'S', 'SS', 0), ('y', 1, 1, 'V', 'SS', 0), ('v', 0, 0, None, 'SS', 0), None, ('y', 2, 1, None, 'SS', 0), ('y', 2, 0, None, 'SS', 0), ('v', 0, 1, None, 'SS', 0), ('v', 1, 0, None, 'SV', 1), ('v', 0, 2, None, 'SV', 0), ('v', 1, 1, 'S', 'SS', 1), None, ('v', 1, 2, 'V', 'SS', 1)]
+        stage2 = {2: ('v', 2, 0, 'S', 'SS', 1), 4: ('v', 2, 1, 'V', 'SS', 1), 13: ('v', 2, 2, 'V', 'SV', 1)}
         pending, late = [], []
         order = [op for op in stage1 if op] + [op for op in stage2.values()]
         turned = []
@@ -264,8 +268,10 @@ def tile_staggered_adoption_weighted_panel_s9_kernel(
             if op:
                 (late if op[5] else pending).append((op, fetch(op, turn(op))))
                 turned.append(op)
-                if len(turned) < len(order):
-                    prep(order[len(turned)])
+
+        def prep_next():
+            if len(turned) < len(order) and order[len(turned)] not in preps:
+                prep(order[len(turned)])
 
         prep(order[0])
         aff = [(g, t) for g in (1, 2) for t in range(4)]
@@ -286,7 +292,8 @@ def tile_staggered_adoption_weighted_panel_s9_kernel(
                 quant(*pending.pop(0))
             start_op(stage1[k])
             if job:
-                affine(*job, mk, "SSSSSSSSSSSS"[k])
+                affine(*job, mk, "SSSSVSSSSSSS"[k])
+            prep_next()
             weigh(g, jb, banks[jb])
             if jb % 4 == 3:
                 ready_e.append((g, jb // 4))
@@ -299,10 +306,11 @@ def tile_staggered_adoption_weighted_panel_s9_kernel(
             bank = second(m, half, "acc" if i < 14 or i % 2 == 0 else "tp")
             if i in stage2:
                 start_op(stage2[i])
+                prep_next()
             if m not in outs:
                 outs[m] = work.tile([P, T], F32, name="o", align_bytes=64, bufs=5)
             cols = slice(512 * half, 512 * (half + 1))
-            copy = nc.scalar.copy if i % 2 == 0 else vec.tensor_copy
+            copy = nc.scalar.copy if "VSSSVSVSSSSSVVSSVVVSSVVS"[i] == "S" else vec.tensor_copy
             copy(out=outs[m][:, cols], in_=bank[:])
             if late or pending:
                 quant(*(pending or late).pop(0))

@@ -35,9 +35,10 @@ def tile_staggered_adoption_weighted_panel_s9_kernel(
         ident = keep.tile([P, P], F32, name="ident")
         ident_bf = keep.tile([P, P], BF16, name="ident_bf")
         dcol = keep.tile([P, 8], BF16, name="dcol")
-        ucol = [keep.tile([P, G, 4], BF16, name=f"ucol{i}") for i in range(3)]
+        rows = keep.tile([P, 512], BF16, name="rows", align_bytes=64)
+        coef = keep.tile([P, 3 * G, 4], F32, name="coef")
         wsc = keep.tile([P, H, T], U8, name="wsc", align_bytes=64)
-        wt = keep.tile([P, H, 2 * T], U8, name="wt", align_bytes=64)
+        wt = [keep.tile([P, H, T], U8, name=f"wt{c}", align_bytes=64) for c in range(2)]
         yraw = [keep.tile([P, 4, T], BF16, name=f"yraw{g}", align_bytes=64) for g in range(G)]
         vraw = [keep.tile([P, 4, UNITS], BF16, name=f"vraw{q}", align_bytes=64) for q in range(3)]
 
@@ -50,32 +51,33 @@ def tile_staggered_adoption_weighted_panel_s9_kernel(
 
         def load_w(c):
             cols = slice(T * c, T * (c + 1))
-            nc.sync.dma_start(out=wt[:, :, cols].bitcast(I32), in_=w_v[:, :, cols].bitcast(I32))
+            nc.sync.dma_start(out=wt[c][:].bitcast(I32), in_=w_v[:, :, cols].bitcast(I32))
 
         def load_v(q, a):
             nc.sync.dma_start(out=vraw[q][:, 2 * a : 2 * a + 2, :], in_=v_v[q, :, 2 * a : 2 * a + 2, :])
 
         vec = nc.vector
-        make_identity(nc, ident[:])
+        nc.gpsimd.memset(rows[:].bitcast(I32), 0)
+        vec.memset(ident[:], 0.0)
+        vec.memset(wsc[:].rearrange("p h n -> p (h n)").bitcast(I32), 0)
+        make_identity(nc, ident[:], nomemset=True)
         nc.scalar.dma_start(out=dcol[:], in_=dates.rearrange("(p m) -> p m", m=8))
         load_y(0, 0, 1)
-        for dst, src, queue in zip(ucol, (starts, treated, control), (nc.scalar, nc.scalar, nc.scalar)):
-            queue.dma_start(out=dst[:], in_=src.rearrange("(g p t) -> p g t", p=P, t=4))
+        for i, vector in enumerate((starts, treated, control)):
+            nc.scalar.dma_start(out=rows[G * i : G * (i + 1), :], in_=vector.rearrange("(g x) -> g x", g=G))
         load_y(0, 1, 2)
-        load_y(0, 2, 3)
-        load_y(0, 3, 4)
-        vec.memset(wsc[:].rearrange("p h n -> p (h n)").bitcast(I32), 0)
+        load_y(0, 2, 4)
+        load_w(0)
         ws_v = w_scales.rearrange("h (q r) n -> r q h n", r=4)
         for r in range(4):
-            nc.scalar.dma_start(out=wsc[r:P:32, :, :].bitcast(I32), in_=ws_v[r].bitcast(I32))
-        load_w(0)
-        load_w(1)
+            nc.sync.dma_start(out=wsc[r:P:32, :, :].bitcast(I32), in_=ws_v[r].bitcast(I32))
         load_y(1, 0, 2)
+        load_w(1)
         load_y(1, 2, 4)
-        load_v(0, 0)
-        load_v(0, 1)
         load_y(2, 0, 2)
         load_y(2, 2, 4)
+        load_v(0, 0)
+        load_v(0, 1)
         for q in (1, 2):
             load_v(q, 0)
             load_v(q, 1)
@@ -84,8 +86,12 @@ def tile_staggered_adoption_weighted_panel_s9_kernel(
         dps = psum.tile([P, 8, P], BF16, name="dps", tag="tp")
         for m in range(8):
             nc.tensor.transpose(dps[:, m, :], dcol[:, m : m + 1].to_broadcast([P, P]), ident_bf[:])
+        rps = psum.tile([P, 4, P], BF16, name="rps", tag="tp")
+        for r in range(4):
+            nc.tensor.transpose(rps[:, r, :], rows[:, r:512:4], ident_bf[:])
         dall = keep.tile([P, T], BF16, name="dall", align_bytes=64)
         vec.tensor_copy(out=dall[:].rearrange("p (j m) -> p j m", m=8), in_=dps[:].rearrange("p m j -> p j m"))
+        vec.tensor_copy(out=coef[:], in_=rps[:, :, 0 : 3 * G].rearrange("p t r -> p r t"))
 
         cw = [keep.tile([P, 4, T], BF16, name=f"cw{g}", align_bytes=64) for g in range(G)]
 
@@ -168,7 +174,7 @@ def tile_staggered_adoption_weighted_panel_s9_kernel(
                             out=banks[jc][:, t, :],
                             lhsT=ycodes[g][:, m].bitcast(E4M3),
                             lhsT_scale=yscales[g][:, m],
-                            rhs=wt[:, h, 256 * jc : 256 * (jc + 1)].bitcast(E2M1),
+                            rhs=wt[jc // 4][:, h, 256 * (jc % 4) : 256 * (jc % 4 + 1)].bitcast(E2M1),
                             rhs_scale=wsc[:, h, P * jc : P * (jc + 1)],
                             start=(h == 0),
                             stop=(h == H - 1),
@@ -179,9 +185,9 @@ def tile_staggered_adoption_weighted_panel_s9_kernel(
                 egrp[g, jc // 4] = work.tile([P, 512, 4], BF16, name="eg", align_bytes=64)
             j = P * (jc % 4)
             vec.tensor_tensor(
-                out=egrp[g, jc // 4][:, j : j + P, :].rearrange("p (c i) t -> p c t i", i=4),
-                in0=bank[:].rearrange("p t (c i) -> p c t i", i=4),
-                in1=cw[g][:, :, P * jc : P * (jc + 1)].rearrange("p t (c i) -> p c t i", i=4),
+                out=egrp[g, jc // 4][:, j : j + P, :].rearrange("p (c i) t -> p c t i", i=2),
+                in0=bank[:].rearrange("p t (c i) -> p c t i", i=2),
+                in1=cw[g][:, :, P * jc : P * (jc + 1)].rearrange("p t (c i) -> p c t i", i=2),
                 op=OP.mult,
             )
 
@@ -211,6 +217,30 @@ def tile_staggered_adoption_weighted_panel_s9_kernel(
         def acc_banks(jcs):
             return {jc: psum.tile([P, 4, P], F32, name="acc") for jc in jcs}
 
+        s_c, t_c, c_c = [coef[:, G * i : G * (i + 1), :].rearrange("p g t -> p (g t)") for i in range(3)]
+
+        def col(name):
+            return keep.tile([P, 4 * G], F32, name=name)
+
+        mags = keep.tile([P, 3 * G, 4], F32, name="mags")
+        diff, flag, thr0, sign, flagn = col("diff"), col("flag"), col("thr0"), col("sign"), col("flagn")
+        part, gain, part2, thr, base = col("part"), col("gain"), col("part2"), col("thr"), col("base")
+        abs_s, abs_t, abs_c = [mags[:, G * i : G * (i + 1), :].rearrange("p g t -> p (g t)") for i in range(3)]
+        vec.tensor_tensor(out=diff[:], in0=t_c, in1=c_c, op=OP.subtract)
+        flat = coef[:].rearrange("p r t -> p (r t)")
+        vec.scalar_tensor_tensor(
+            out=mags[:].rearrange("p r t -> p (r t)"), in0=flat, scalar=-1.0, in1=flat, op0=OP.mult, op1=OP.max
+        )
+        vec.tensor_tensor(out=flag[:], in0=abs_t, in1=abs_c, op=OP.is_ge)
+        vec.scalar_tensor_tensor(out=thr0[:], in0=abs_s, scalar=-(2.0**-10), in1=s_c, op0=OP.mult, op1=OP.add)
+        vec.tensor_scalar(out=sign[:], in0=flag[:], scalar1=2.0, scalar2=-1.0, op0=OP.mult, op1=OP.add)
+        vec.tensor_scalar(out=flagn[:], in0=flag[:], scalar1=-1.0, scalar2=1.0, op0=OP.mult, op1=OP.add)
+        vec.tensor_tensor(out=part[:], in0=flag[:], in1=c_c, op=OP.mult)
+        vec.tensor_tensor(out=gain[:], in0=diff[:], in1=sign[:], op=OP.mult)
+        vec.tensor_tensor(out=part2[:], in0=flagn[:], in1=t_c, op=OP.mult)
+        vec.scalar_tensor_tensor(out=thr[:], in0=thr0[:], scalar=-(2.0**-120), in1=sign[:], op0=OP.add, op1=OP.mult)
+        vec.tensor_tensor(out=base[:], in0=part[:], in1=part2[:], op=OP.add)
+
         banks = acc_banks(range(4))
         src = yraw[0][:].bitcast(F32)
         grp0 = []
@@ -228,38 +258,18 @@ def tile_staggered_adoption_weighted_panel_s9_kernel(
             first(0, range(4), (t,), banks)
 
         quant0(0)
-        s_c, t_c, c_c = [u[:].rearrange("p g t -> p (g t)") for u in ucol]
-
-        def col(name):
-            return keep.tile([P, 4 * G], F32, name=name)
-
-        abs_t, abs_c, abs_s = col("abs_t"), col("abs_c"), col("abs_s")
-        diff, flag, thr0, sign, flagn = col("diff"), col("flag"), col("thr0"), col("sign"), col("flagn")
-        part, gain, part2, thr, base = col("part"), col("gain"), col("part2"), col("thr"), col("base")
-        for dst, src in ((abs_s, s_c), (abs_t, t_c), (abs_c, c_c)):
-            vec.scalar_tensor_tensor(out=dst[:], in0=src, scalar=-1.0, in1=src, op0=OP.mult, op1=OP.max)
-        vec.tensor_tensor(out=diff[:], in0=t_c, in1=c_c, op=OP.subtract)
-        vec.tensor_tensor(out=flag[:], in0=abs_t[:], in1=abs_c[:], op=OP.is_ge)
-        vec.scalar_tensor_tensor(out=thr0[:], in0=abs_s[:], scalar=-(2.0**-10), in1=s_c, op0=OP.mult, op1=OP.add)
-        vec.tensor_scalar(out=sign[:], in0=flag[:], scalar1=2.0, scalar2=-1.0, op0=OP.mult, op1=OP.add)
-        vec.tensor_scalar(out=flagn[:], in0=flag[:], scalar1=-1.0, scalar2=1.0, op0=OP.mult, op1=OP.add)
-        vec.tensor_tensor(out=part[:], in0=flag[:], in1=c_c, op=OP.mult)
-        vec.tensor_tensor(out=gain[:], in0=diff[:], in1=sign[:], op=OP.mult)
-        vec.tensor_tensor(out=part2[:], in0=flagn[:], in1=t_c, op=OP.mult)
-        vec.scalar_tensor_tensor(out=thr[:], in0=thr0[:], scalar=-(2.0**-120), in1=sign[:], op0=OP.add, op1=OP.mult)
-        vec.tensor_tensor(out=base[:], in0=part[:], in1=part2[:], op=OP.add)
         quant0(1)
         m0, m1 = mask(0, 0), mask(0, 1)
         affine(0, 0, m0, "V")
-        affine(0, 1, m1, "S")
+        affine(0, 1, m1, "V")
         quant0(2)
         m2, m3 = mask(0, 2), mask(0, 3)
         quant0(3)
-        affine(0, 2, m2, "V")
+        affine(0, 2, m2, "S")
         affine(0, 3, m3, "V")
 
-        stage1 = [('y', 1, 0, 'S', 'SS', 0), ('y', 1, 1, 'V', 'SS', 0), ('v', 0, 0, None, 'SS', 0), None, ('y', 2, 1, None, 'SS', 0), ('y', 2, 0, None, 'SS', 0), ('v', 0, 1, None, 'SS', 0), ('v', 1, 0, None, 'SV', 1), ('v', 0, 2, None, 'SV', 0), ('v', 1, 1, 'S', 'SS', 1), None, ('v', 1, 2, 'V', 'SS', 1)]
-        stage2 = {2: ('v', 2, 0, 'S', 'SS', 1), 4: ('v', 2, 1, 'V', 'SS', 1), 13: ('v', 2, 2, 'V', 'SV', 1)}
+        stage1 = [('y', 1, 0, 'V', 'SS', 0), ('y', 1, 1, None, 'SS', 0), ('y', 2, 1, None, 'SS', 0), ('v', 0, 1, None, 'SS', 0), ('v', 0, 0, None, 'SS', 0), ('y', 2, 0, None, 'SS', 0), ('v', 1, 0, None, 'SV', 1), None, ('v', 1, 2, 'S', 'SS', 0), ('v', 0, 2, None, 'SS', 0), None, ('v', 1, 1, 'S', 'SS', 1)]
+        stage2 = {1: ('v', 2, 0, 'V', 'SV', 1), 7: ('v', 2, 1, 'S', 'SS', 1), 12: ('v', 2, 2, 'S', 'SV', 1)}
         pending, late = [], []
         order = [op for op in stage1 if op] + [op for op in stage2.values()]
         turned = []
@@ -292,7 +302,7 @@ def tile_staggered_adoption_weighted_panel_s9_kernel(
                 quant(*pending.pop(0))
             start_op(stage1[k])
             if job:
-                affine(*job, mk, "SSSSVSSSSSSS"[k])
+                affine(*job, mk, "VSSVSSSSSSSS"[k])
             prep_next()
             weigh(g, jb, banks[jb])
             if jb % 4 == 3:
@@ -310,7 +320,7 @@ def tile_staggered_adoption_weighted_panel_s9_kernel(
             if m not in outs:
                 outs[m] = work.tile([P, T], F32, name="o", align_bytes=64, bufs=5)
             cols = slice(512 * half, 512 * (half + 1))
-            copy = nc.scalar.copy if "VSSSVSVSSSSSVVSSVVVSSVVS"[i] == "S" else vec.tensor_copy
+            copy = nc.scalar.copy if "VSVSVVVVVSSSVVVVSSSSVSSS"[i] == "S" else vec.tensor_copy
             copy(out=outs[m][:, cols], in_=bank[:])
             if late or pending:
                 quant(*(pending or late).pop(0))

from contextlib import ExitStack

import concourse.mybir as mybir
from concourse.masks import make_identity

UNITS, T = 1536, 1024
FLOPS = 2 * UNITS * T * T + 2 * UNITS * UNITS * T

F32 = mybir.dt.float32
BF16 = mybir.dt.bfloat16
U32 = mybir.dt.uint32
I32 = mybir.dt.int32
U8 = mybir.dt.uint8
E4M3 = mybir.dt.float8_e4m3fn_x4
E5M2 = mybir.dt.float8_e5m2_x4
E2M1 = mybir.dt.float4_e2m1fn_x4
OP = mybir.AluOpType
ACT = mybir.ActivationFunctionType

P = 128
G = UNITS // 512
H = T // 512


def tile_staggered_adoption_weighted_panel_s9_kernel(
    tc, y, w_words, w_scales, v, dates, starts, treated, control, out
):
    nc = tc.nc
    with ExitStack() as ctx:
        keep = ctx.enter_context(tc.tile_pool(name="keep", bufs=1))
        work = ctx.enter_context(tc.tile_pool(name="work", bufs=3))
        psum = ctx.enter_context(tc.psum_pool(name="psum", bufs=4))
        ctx.enter_context(tc.manual_schedule())

        ident = keep.tile([P, P], F32, name="ident")
        ident_bf = keep.tile([P, P], BF16, name="ident_bf")
        dcol = keep.tile([P, 8], BF16, name="dcol")
        rows = keep.tile([P, 512], BF16, name="rows", align_bytes=64)
        coef = keep.tile([P, 3 * G, 4], F32, name="coef")
        wsc = keep.tile([P, H, T], U8, name="wsc", align_bytes=64)
        wt = [keep.tile([P, H, T], U8, name=f"wt{c}", align_bytes=64) for c in range(2)]
        yraw = [keep.tile([P, 4, T], BF16, name=f"yraw{g}", align_bytes=64) for g in range(G)]
        vraw = [keep.tile([P, 4, UNITS], BF16, name=f"vraw{q}", align_bytes=64) for q in range(3)]

        y_v = y.rearrange("(g p t) k -> g p t k", p=P, t=4)
        v_v = v.rearrange("(q m p) k -> q p m k", p=P, m=4)
        w_v = w_words.rearrange("h p n -> p h n")

        def load_y(g, t0, t1):
            nc.sync.dma_start(out=yraw[g][:, t0:t1, :], in_=y_v[g, :, t0:t1, :])

        def load_w(c):
            cols = slice(T * c, T * (c + 1))
            nc.sync.dma_start(out=wt[c][:].bitcast(I32), in_=w_v[:, :, cols].bitcast(I32))

        def load_v(q, a):
            nc.sync.dma_start(out=vraw[q][:, 2 * a : 2 * a + 2, :], in_=v_v[q, :, 2 * a : 2 * a + 2, :])

        vec = nc.vector
        nc.gpsimd.memset(rows[:].bitcast(I32), 0)
        vec.memset(ident[:], 0.0)
        vec.memset(wsc[:].rearrange("p h n -> p (h n)").bitcast(I32), 0)
        make_identity(nc, ident[:], nomemset=True)
        nc.scalar.dma_start(out=dcol[:], in_=dates.rearrange("(p m) -> p m", m=8))
        load_y(0, 0, 1)
        for i, vector in enumerate((starts, treated, control)):
            nc.scalar.dma_start(out=rows[G * i : G * (i + 1), :], in_=vector.rearrange("(g x) -> g x", g=G))
        load_y(0, 1, 2)
        load_y(0, 2, 4)
        load_w(0)
        ws_v = w_scales.rearrange("h (q r) n -> r q h n", r=4)
        for r in range(4):
            nc.sync.dma_start(out=wsc[r:P:32, :, :].bitcast(I32), in_=ws_v[r].bitcast(I32))
        load_y(1, 0, 2)
        load_w(1)
        load_y(1, 2, 4)
        load_y(2, 0, 2)
        load_y(2, 2, 4)
        load_v(0, 0)
        load_v(0, 1)
        for q in (1, 2):
            load_v(q, 0)
            load_v(q, 1)

        vec.tensor_copy(out=ident_bf[:], in_=ident[:])
        dps = psum.tile([P, 8, P], BF16, name="dps", tag="tp")
        for m in range(8):
            nc.tensor.transpose(dps[:, m, :], dcol[:, m : m + 1].to_broadcast([P, P]), ident_bf[:])
        rps = psum.tile([P, 4, P], BF16, name="rps", tag="tp")
        for r in range(4):
            nc.tensor.transpose(rps[:, r, :], rows[:, r:512:4], ident_bf[:])
        dall = keep.tile([P, T], BF16, name="dall", align_bytes=64)
        vec.tensor_copy(out=dall[:].rearrange("p (j m) -> p j m", m=8), in_=dps[:].rearrange("p m j -> p j m"))
        vec.tensor_copy(out=coef[:], in_=rps[:, :, 0 : 3 * G].rearrange("p t r -> p r t"))

        cw = [keep.tile([P, 4, T], BF16, name=f"cw{g}", align_bytes=64) for g in range(G)]

        def mask(g, t):
            i = 4 * g + t
            mk = work.tile([P, T], BF16, name="mk", align_bytes=64)
            vec.tensor_scalar(
                out=mk[:], in0=dall[:], scalar1=sign[:, i : i + 1], scalar2=thr[:, i : i + 1], op0=OP.mult, op1=OP.is_ge
            )
            return mk

        def affine(g, t, mk, engine):
            i = 4 * g + t
            dst, ga, ba = cw[g][:, t, :], gain[:, i : i + 1], base[:, i : i + 1]
            if engine == "V":
                vec.tensor_scalar(out=dst, in0=mk[:], scalar1=ga, scalar2=ba, op0=OP.mult, op1=OP.add)
            else:
                nc.scalar.activation(out=dst, in_=mk[:], func=ACT.Identity, bias=ba, scale=ga)

        ycodes = [keep.tile([P, 2048 // 2], U32, name=f"yc{g}", align_bytes=64) for g in range(G)]
        yscales = [keep.tile([P, 2048 // 2], U8, name=f"ys{g}", align_bytes=64) for g in range(G)]
        vcodes, ecodes, egrp, preps = {}, {}, {}, {}

        def blocks(op):
            kind, i, j = op[:3]
            if kind == "y":
                return yraw[i][:].bitcast(F32)[:, 2 * j : 2 * j + 2, :].rearrange("p t (h k) -> p (t h) k", h=H)
            return vraw[i][:].bitcast(F32)[:, :, 256 * j : 256 * (j + 1)]

        def prep(op):
            engine = op[3]
            if engine:
                ordered = work.tile([P, 4, 2, P], F32, name="ordered", align_bytes=64, bufs=2)
                copy = vec.tensor_copy if engine == "V" else nc.scalar.copy
                copy(out=ordered[:], in_=blocks(op).rearrange("p s (w u) -> p s u w", u=2))
                preps[op] = ordered

        def turn(op):
            banks = []
            src = blocks(op)
            for b in range(2):
                bank = psum.tile([P, 512], F32, name="tp")
                for s in range(2):
                    for u in range(2):
                        words = preps[op][:, 2 * b + s, u, :] if op in preps else src[:, 2 * b + s, u:256:2]
                        nc.tensor.transpose(bank[:, P * (2 * s + u) : P * (2 * s + u + 1)], words, ident[:])
                banks.append(bank)
            return banks

        def fetch_bank(dst, bank, engine):
            copy = vec.tensor_copy if engine == "V" else nc.scalar.copy
            copy(
                out=dst.bitcast(F32).rearrange("p (a r u) -> p a r u", a=2, u=2),
                in_=bank[:].rearrange("p (a u r) -> p a r u", a=2, u=2),
            )

        def fetch(op, banks):
            grp = work.tile([P, 2048], BF16, name="grp", align_bytes=64, bufs=6)
            for b in range(2):
                fetch_bank(grp[:, 1024 * b : 1024 * (b + 1)], banks[b], op[4][b])
            return grp

        def quant(op, grp):
            kind, i, j = op[:3]
            if kind == "y":
                codes, scales = ycodes[i][:, 512 * j : 512 * (j + 1)], yscales[i][:, 512 * j : 512 * (j + 1)]
            else:
                ct = keep.tile([P, 512], U32, name=f"vc{i}{j}", align_bytes=64)
                st = keep.tile([P, 512], U8, name=f"vs{i}{j}", align_bytes=64)
                vcodes[i, j] = (ct, st)
                codes, scales = ct[:], st[:]
            vec.quantize_mx(out=codes.bitcast(E4M3), scales=scales, in_=grp[:])

        def first(g, jcs, ts, banks):
            for t in ts:
                for jc in jcs:
                    for h in range(H):
                        m = slice(256 * t + P * h, 256 * t + P * (h + 1))
                        nc.tensor.matmul_mx(
                            out=banks[jc][:, t, :],
                            lhsT=ycodes[g][:, m].bitcast(E4M3),
                            lhsT_scale=yscales[g][:, m],
                            rhs=wt[jc // 4][:, h, 256 * (jc % 4) : 256 * (jc % 4 + 1)].bitcast(E2M1),
                            rhs_scale=wsc[:, h, P * jc : P * (jc + 1)],
                            start=(h == 0),
                            stop=(h == H - 1),
                        )

        def weigh(g, jc, bank):
            if jc % 4 == 0:
                egrp[g, jc // 4] = work.tile([P, 512, 4], BF16, name="eg", align_bytes=64)
            j = P * (jc % 4)
            vec.tensor_tensor(
                out=egrp[g, jc // 4][:, j : j + P, :].rearrange("p (c i) t -> p c t i", i=2),
                in0=bank[:].rearrange("p t (c i) -> p c t i", i=2),
                in1=cw[g][:, :, P * jc : P * (jc + 1)].rearrange("p t (c i) -> p c t i", i=2),
                op=OP.mult,
            )

        def quant_e(g, half):
            ct = keep.tile([P, 512], U32, name=f"ec{g}{half}", align_bytes=64)
            st = keep.tile([P, 512], U8, name=f"es{g}{half}", align_bytes=64)
            ecodes[g, half] = (ct, st)
            vec.quantize_mx(out=ct[:].bitcast(E5M2), scales=st[:], in_=egrp[g, half][:].rearrange("p n t -> p (n t)"))

        def second(m, half, tag):
            q, mi = m // 4, m % 4
            bank = psum.tile([P, 512], F32, name="bank2", tag=tag)
            for g in range(G):
                codes, scales = vcodes[q, g]
                ec, es = ecodes[g, half]
                nc.tensor.matmul_mx(
                    out=bank[:],
                    lhsT=codes[:, P * mi : P * (mi + 1)].bitcast(E4M3),
                    lhsT_scale=scales[:, P * mi : P * (mi + 1)],
                    rhs=ec[:].bitcast(E5M2),
                    rhs_scale=es[:],
                    start=(g == 0),
                    stop=(g == G - 1),
                )
            return bank

        def acc_banks(jcs):
            return {jc: psum.tile([P, 4, P], F32, name="acc") for jc in jcs}

        s_c, t_c, c_c = [coef[:, G * i : G * (i + 1), :].rearrange("p g t -> p (g t)") for i in range(3)]

        def col(name):
            return keep.tile([P, 4 * G], F32, name=name)

        mags = keep.tile([P, 3 * G, 4], F32, name="mags")
        diff, flag, thr0, sign, flagn = col("diff"), col("flag"), col("thr0"), col("sign"), col("flagn")
        part, gain, part2, thr, base = col("part"), col("gain"), col("part2"), col("thr"), col("base")
        abs_s, abs_t, abs_c = [mags[:, G * i : G * (i + 1), :].rearrange("p g t -> p (g t)") for i in range(3)]
        vec.tensor_tensor(out=diff[:], in0=t_c, in1=c_c, op=OP.subtract)
        flat = coef[:].rearrange("p r t -> p (r t)")
        vec.scalar_tensor_tensor(
            out=mags[:].rearrange("p r t -> p (r t)"), in0=flat, scalar=-1.0, in1=flat, op0=OP.mult, op1=OP.max
        )
        vec.tensor_tensor(out=flag[:], in0=abs_t, in1=abs_c, op=OP.is_ge)
        vec.scalar_tensor_tensor(out=thr0[:], in0=abs_s, scalar=-(2.0**-10), in1=s_c, op0=OP.mult, op1=OP.add)
        vec.tensor_scalar(out=sign[:], in0=flag[:], scalar1=2.0, scalar2=-1.0, op0=OP.mult, op1=OP.add)
        vec.tensor_scalar(out=flagn[:], in0=flag[:], scalar1=-1.0, scalar2=1.0, op0=OP.mult, op1=OP.add)
        vec.tensor_tensor(out=part[:], in0=flag[:], in1=c_c, op=OP.mult)
        vec.tensor_tensor(out=gain[:], in0=diff[:], in1=sign[:], op=OP.mult)
        vec.tensor_tensor(out=part2[:], in0=flagn[:], in1=t_c, op=OP.mult)
        vec.scalar_tensor_tensor(out=thr[:], in0=thr0[:], scalar=-(2.0**-120), in1=sign[:], op0=OP.add, op1=OP.mult)
        vec.tensor_tensor(out=base[:], in0=part[:], in1=part2[:], op=OP.add)

        banks = acc_banks(range(4))
        src = yraw[0][:].bitcast(F32)
        grp0 = []
        for t in range(4):
            tb = psum.tile([P, 512], F32, name="tp")
            for s in range(4):
                h, u = s // 2, s % 2
                nc.tensor.transpose(tb[:, P * s : P * (s + 1)], src[:, t, 256 * h + u : 256 * (h + 1) : 2], ident[:])
            gt = work.tile([P, 1024], BF16, name="grp0", align_bytes=64, bufs=4)
            fetch_bank(gt[:], tb, "SSSS"[t])
            grp0.append(gt)
        def quant0(t):
            cols = slice(256 * t, 256 * (t + 1))
            vec.quantize_mx(out=ycodes[0][:, cols].bitcast(E4M3), scales=yscales[0][:, cols], in_=grp0[t][:])
            first(0, range(4), (t,), banks)

        quant0(0)
        quant0(1)
        m0, m1 = mask(0, 0), mask(0, 1)
        affine(0, 0, m0, "V")
        affine(0, 1, m1, "V")
        quant0(2)
        m2, m3 = mask(0, 2), mask(0, 3)
        quant0(3)
        affine(0, 2, m2, "S")
        affine(0, 3, m3, "V")

        stage1 = [('y', 1, 0, 'V', 'SS', 0), ('y', 1, 1, None, 'SS', 0), ('y', 2, 1, None, 'SS', 0), ('v', 0, 1, None, 'SS', 0), ('v', 0, 0, None, 'SS', 0), ('y', 2, 0, None, 'SS', 0), ('v', 1, 0, None, 'SV', 1), None, ('v', 1, 2, 'S', 'SS', 0), ('v', 0, 2, None, 'SS', 0), None, ('v', 1, 1, 'S', 'SS', 1)]
        stage2 = {1: ('v', 2, 0, 'V', 'SV', 1), 7: ('v', 2, 1, 'S', 'SS', 1), 12: ('v', 2, 2, 'S', 'SV', 1)}
        pending, late = [], []
        order = [op for op in stage1 if op] + [op for op in stage2.values()]
        turned = []

        def start_op(op):
            if op:
                (late if op[5] else pending).append((op, fetch(op, turn(op))))
                turned.append(op)

        def prep_next():
            if len(turned) < len(order) and order[len(turned)] not in preps:
                prep(order[len(turned)])

        prep(order[0])
        aff = [(g, t) for g in (1, 2) for t in range(4)]
        groups = [(0, (0, 1)), (0, (2, 3)), (0, (4, 5)), (0, (6, 7))] + [(g, (j, j + 1)) for g in (1, 2) for j in (0, 2, 4, 6)]
        ready_e = []
        for k, (g, (ja, jb)) in enumerate(groups):
            if k >= 2:
                banks = acc_banks((ja, jb))
                first(g, (ja,), range(4), banks)
                first(g, (jb,), range(4), banks)
            job = aff.pop(0) if aff else None
            if job:
                mk = mask(*job)
            weigh(g, ja, banks[ja])
            if ready_e:
                quant_e(*ready_e.pop())
            if pending:
                quant(*pending.pop(0))
            start_op(stage1[k])
            if job:
                affine(*job, mk, "VSSVSSSSSSSS"[k])
            prep_next()
            weigh(g, jb, banks[jb])
            if jb % 4 == 3:
                ready_e.append((g, jb // 4))
        quant_e(*ready_e.pop())

        out_v = out.rearrange("(m p) j -> m p j", p=P)
        outs = {}
        steps = [(m, half) for mp in range(6) for half in range(2) for m in (2 * mp, 2 * mp + 1)]
        for i, (m, half) in enumerate(steps):
            bank = second(m, half, "acc" if i < 14 or i % 2 == 0 else "tp")
            if i in stage2:
                start_op(stage2[i])
                prep_next()
            if m not in outs:
                outs[m] = work.tile([P, T], F32, name="o", align_bytes=64, bufs=5)
            cols = slice(512 * half, 512 * (half + 1))
            copy = nc.scalar.copy if "VSVSVVVVVSSSVVVVSSSSVSSS"[i] == "S" else vec.tensor_copy
            copy(out=outs[m][:, cols], in_=bank[:])
            if late or pending:
                quant(*(pending or late).pop(0))
            if m >= 10:
                nc.sync.dma_start(out=out_v[m, :, cols], in_=outs[m][:, cols])
            elif half == 1:
                nc.sync.dma_start(out=out_v[m], in_=outs[m][:])
